import numpy as np, ml_dtypes
CORES = [5,29,101,125,133,157,229,253]
N = 8
BF = ml_dtypes.bfloat16
def gentries(a):
    return np.ascontiguousarray(a.reshape(8, 16, -1).transpose(0, 2, 1)).reshape(8, -1)
def gtable(e):
    e = np.asarray(e); return np.ascontiguousarray(e.reshape(8, -1, 16).transpose(0, 2, 1)).reshape(128, -1).astype(np.int32)
S, C, B, U, RO, Q = 2048, 2048, 96, 32, 3, 10
L = B + U
def parts(rng):
    sk = (256 * (0.25 + 0.75 * rng.random((N, 8, 1, C))) * rng.random((N, 8, 16, C))).astype(np.int64); sk = np.minimum(sk, 255); sk[..., C - 1] = 0
    oc = np.where(rng.random((N, 8, S)) < 0.05, C - 1, rng.integers(0, C - 1, (N, 8, S)))
    cv = rng.integers(0, S, (N, 8, 16, S)); cd = np.ascontiguousarray(np.argsort(rng.random((N, 8, RO, S)), axis=-1)[..., :L * 16])
    return sk, oc, cv, cd
def fill(rng, share):
    u = rng.random((N, 8, 1, RO, B)); v = rng.random((N, 8, 1, RO, B))
    h = np.where(u < share, 9 + 31 * v, np.where(u < share + 0.1, 4 + 5 * v, np.where(u < share + 0.3, 0.0, 0.2 + 3.8 * v)))
    w = rng.random((N, 8, 16, RO, B)) * (rng.random((N, 8, 16, RO, B)) < 0.7)
    return np.minimum((80 * h * w).astype(np.int64), 4096)
def sums(sk, oc, cd):
    who = np.take_along_axis(oc, cd[:, :, 0, :B * 16], 2)
    return np.add.accumulate(np.take_along_axis(sk, who[:, :, None, :], 3).reshape(N, 8, 16, B, 16), axis=4)
def heavy(rng, sk, oc, cv, cd, nd):
    own = np.arange(S); j = np.arange(B)
    for g in rng.permutation(8)[:2]:
        left = []
        for q in range(N):
            v = rng.integers(200, 256, (16, C)); v[:, C - 1] = 0; e = rng.integers(L, C - 1, S)
            st = cd[q, g, 0].reshape(L, 16); late = st[B:].reshape(-1)
            cd[q, g, 1] = np.concatenate([rng.permutation(st[:B].reshape(-1)), rng.permutation(late)])
            cv[q, g] = rng.choice(np.setdiff1d(own, late), (16, S))
            p = rng.integers(10, 16, B); before = np.add.accumulate(v[:, e[st[:B]]], axis=2)[:, j, p - 1]
            x = 208 + (-before) % 16; want = before + x
            x[rng.integers(0, 16, B), j] -= rng.integers(0, 2, B)
            v[:, :B] = x; e[st[j, p]] = j
            big = rng.permutation(B)[:U // 2]; e[st[big[U // 8:], 8:]] = C - 1
            want[:, big] = 0; want[rng.integers(0, 16, U // 2), big] = 4096
            sk[q, g] = v; oc[q, g] = e; nd[q, g] = 0; nd[q, g, :, 0] = want
            end = np.add.reduce(v[:, e[st[:B]]], axis=2); u = np.nonzero(np.any(end < want, axis=0))[0][:U]
            left.append(np.maximum(want[:, u] - end[:, u], 0))
        for q in range(N):
            w = left[q - 1]; n = w.shape[1]; k = np.arange(n); z = np.argmax(w, axis=0); top = w[z, k]
            st = cd[q, g, 1].reshape(L, 16)[B:B + n]
            line = np.add.accumulate(sk[q, g][z[:, None], oc[q, g][st]], axis=1)
            p = np.add.reduce((line < top[:, None]).astype(np.int64), axis=1)
            before = np.where(p > 0, line[k, np.maximum(p - 1, 0)], 0)
            sk[q, g, z, B + k] = top - before - k % 2; oc[q, g, st[k, p]] = B + k
def pack(sk, oc, cv, cd, nd):
    return {"skill": np.ascontiguousarray(sk.reshape(N, 128, C)).astype(np.float32).astype(BF), "occ": oc.astype(np.int32), "cover": np.ascontiguousarray(cv.reshape(N, 128, S)).astype(np.int32),
            "cards": np.stack([gtable(a.reshape(8, -1)) for a in cd]), "need": np.ascontiguousarray(nd.reshape(N, 128, RO * B)).astype(np.float32).astype(BF)}
def setup_inputs(rng):
    sk, oc, cv, cd = parts(rng)
    return pack(sk, oc, cv, cd, fill(rng, rng.choice(np.array([0.03, 0.1, 0.2, 0.3]), (N, 8, 1, 1, 1))))
def setup_inputs_room(rng):
    sk, oc, cv, cd = parts(rng); nd = np.zeros((N, 8, 16, RO, B), np.int64); pre = sums(sk, oc, cd)
    nd[:, :, :, 0] = pre[..., 0] * (rng.random((N, 8, 1, B)) < 0.5)
    for q in range(N):
        for t in range(RO):
            size = rng.permutation(np.array([0, 1, U - 1, U, U + 1, B, U, 0]))
            for g in range(8):
                n = int(size[g]); lanes = rng.permutation(B)[:n]
                nd[q, g, :, t, lanes] = rng.integers(0, 256, (n, 16)); nd[q, g, rng.integers(0, 16, n), t, lanes] = 4096
    return pack(sk, oc, cv, cd, nd)
def setup_inputs_ties(rng):
    sk, oc, cv, cd = parts(rng)
    few = rng.integers(0, 3, sk.shape) * 16; m = np.arange(8)[None, :, None, None] % 2 == 0
    sk = np.where(m, few, sk // 16 * 16) * (rng.random((N, 8, 1, C)) > 0.1); sk[..., C - 1] = 0
    nd = fill(rng, 0.05); pre = sums(sk, oc, cd)
    p = rng.choice(np.array([0, 0, 1, 3, 7, 14, 15, 15]), (N, 8, B))
    w = np.take_along_axis(pre, p[:, :, None, :, None], 4)[..., 0]
    w = w + 16 * ((np.arange(16)[None, None, :, None] == rng.integers(0, 16, (N, 8, 1, B))) & (rng.random((N, 8, 1, B)) < 0.5))
    nd[:, :, :, 0] = w * (rng.random((N, 8, 1, B)) > 0.3)
    heavy(rng, sk, oc, cv, cd, nd)
    return pack(sk, oc, cv, cd, nd)
def setup_inputs_crowd(rng):
    sk, oc, cv, cd = parts(rng); h = B // 2; sk[..., 0] = 255; own = np.arange(S); o = rng.permutation(8)
    full = np.argsort(rng.random((N, 8, B)), axis=-1)[..., :U]
    for q in range(N):
        for g in range(8):
            card = cd[q, g, 0].reshape(L, 16)
            if g == o[0] or g == o[1]:
                k = rng.permutation(np.setdiff1d(own, card[full[q, g]].reshape(-1))); a, b = k[:L], k[L:2 * L]
                mid = rng.permutation(np.setdiff1d(own, k[:2 * L]))[:14 * L].reshape(L, 14)
                cd[q, g, 1] = np.concatenate([a[:, None], mid, b[:, None]], axis=1).reshape(-1)
                v = np.clip(sk[q, g], 16, 239); v[:, :16] = rng.integers(240, 256, (16, 16)); v[:, C - 1] = 0; sk[q, g] = v
                oc[q, g, a] = rng.integers(16, C - 1, L); oc[q, g, b] = rng.integers(0, 16, L)
                c = np.repeat(own[None, :], 16, axis=0)
                if g == o[0]: c[:, a] = b[rng.integers(0, 2, (16, L))]
                else: c[:, a] = np.where(np.arange(16)[:, None] >= rng.integers(0, 16, L)[None, :], b[None, :], a[None, :])
                cv[q, g] = c
            else:
                pool = card[h:h + 16, 15]; oc[q, g, pool[:8]] = 0
                c = pool[rng.integers(0, 16, (16, S))]; kind = rng.integers(0, 5, S)
                c[:15] = np.where(kind >= 3, own, c[:15]); c[15] = np.where(kind == 4, own, c[15]); cv[q, g] = c
    nd = fill(rng, 0.05); pre = sums(sk, oc, cd)
    nd[:, :, :, 0] = pre[..., 0] * (np.arange(B) < h); nd[:, o[:2]] = 0
    for q in range(N):
        for g in o[:2]:
            z = rng.integers(0, 16, U); l = full[q, g]; nd[q, g, z, 0, l] = pre[q, g, z, l, 15] // 16 * 16 + 16
            nd[q, g, rng.integers(0, 16, B), 1, np.arange(B)] = rng.integers(1, 17, B)
    return pack(sk, oc, cv, cd, nd)
def setup_inputs_bare(rng):
    sk, oc, cv, cd = parts(rng); h = rng.permutation(8)
    oc = np.where(rng.random((N, 8, S)) < rng.choice(np.array([0.4, 0.6, 0.8]), (N, 8, 1)), C - 1, oc); oc[:, h[0]] = C - 1
    ends = np.array([0, 1, S - 2, S - 1]); cv[:, h[2]] = rng.choice(ends, (N, 16, S)); oc[:, h[2], :2] = rng.integers(0, C - 1, (N, 2)); oc[:, h[2], S - 2:] = rng.integers(0, C - 1, (N, 2))
    nd = fill(rng, 0.05) * (rng.random((N, 8, 1, RO, B)) < 0.5); nd[::2, h[1]] = 0
    return pack(sk, oc, cv, cd, nd)
def setup_inputs_spread(rng):
    sk, oc, cv, cd = parts(rng)
    sk = np.minimum((np.exp2(8.2 * rng.random((N, 8, 1, C))) * rng.random((N, 8, 16, C))).astype(np.int64), 255); sk[..., C - 1] = 0
    oc = np.where(rng.random((N, 8, S)) < 0.1, C - 1, np.minimum(((C - 1) * rng.random((N, 8, S)) ** 3).astype(np.int64), C - 2))
    cv = np.minimum((S * rng.random((N, 8, 16, S)) ** 2).astype(np.int64), S - 1)
    nd = (np.minimum(np.exp2(12.2 * rng.random((N, 8, 1, RO, B))), 4096) * rng.choice(np.array([0.0, 0.25, 0.5, 1.0]), (N, 8, 16, RO, B))).astype(np.int64)
    return pack(sk, oc, cv, cd, nd * (rng.random((N, 8, 1, RO, B)) > 0.3))
def check_inputs(d):
    bad = []
    for k, hi in (("skill", 255), ("need", 4096), ("occ", C - 1), ("cover", S - 1), ("cards", S - 1)):
        x = np.asarray(d[k]).astype(np.float64)
        if not np.all((x >= 0) & (x <= hi) & (x == np.floor(x))): bad.append("range of " + k)
    if not np.all(np.asarray(d["skill"])[:, :, C - 1].astype(np.float32) == 0): bad.append("last column of skill")
    e = np.sort(np.asarray(d["cards"]).reshape(N, 8, 16, RO, L).transpose(0, 1, 3, 2, 4).reshape(N, 8, RO, 16 * L), axis=-1)
    if np.any(e[..., 1:] == e[..., :-1]): bad.append("equal stations on the cards of a round")
    return bad
def reference(skill, occ, cover, cards, need):
    sk = skill.astype(np.float32).astype(np.int64).reshape(N, 8, 16, C); cv = cover.astype(np.int64).reshape(N, 8, 16, S)
    cd = np.stack([gentries(a) for a in cards]).astype(np.int64).reshape(N, 8, RO, L, 16); nd = need.astype(np.float32).astype(np.int64).reshape(N, 8, 16, RO, B)
    oc = np.array(occ, dtype=np.int64); arrived = np.zeros((N, 8, 16, U), np.int64)
    for t in range(RO):
        sent = np.zeros((N, 8, 16, U), np.int64)
        for r in range(N):
            w = np.concatenate([nd[r, :, :, t], arrived[r]], axis=2)
            st = cd[r, :, t]; flat = st.reshape(8, -1)
            who = np.take_along_axis(oc[r], flat, 1)
            col = np.take_along_axis(sk[r], who[:, None, :], 2).reshape(8, 16, L, 16)
            pre = np.add.accumulate(col, axis=3)
            met = np.all(pre >= w[..., None], axis=1)
            zero = np.all(w == 0, axis=1)
            leave = ~np.concatenate([zero[..., None], met[..., :15]], axis=2)
            unmet = ~met[..., 15]; before = np.add.accumulate(unmet.astype(np.int64), axis=1) - unmet
            rest = np.maximum(w - pre[..., 15], 0); g, l = np.nonzero(unmet & (before < U))
            sent[(r + 1) % N][g, :, before[g, l]] = rest[g, :, l]
            np.put_along_axis(oc[r], flat, np.where(leave.reshape(8, -1), C - 1, who), 1)
            s = st[..., 0]; lost = leave[..., 0] & (who.reshape(8, L, 16)[..., 0] != C - 1)
            m = np.take_along_axis(cv[r], s[:, None, :], 2)
            a = np.take_along_axis(oc[r], m.reshape(8, -1), 1)
            ka = np.take_along_axis(sk[r], a[:, None, :], 2).reshape(8, 16, 16, L)
            a = a.reshape(8, 16, L); good = np.add.reduce((ka >= col[:, :, None, :, 0]).astype(np.int64), axis=1)
            fit = (a != C - 1) & (good >= Q); ok = lost & np.any(fit, axis=1)
            i = np.argmax(fit, axis=1)[:, None, :]
            src = np.take_along_axis(m, i, 1)[:, 0]; new = np.take_along_axis(a, i, 1)[:, 0]
            for g in range(8):
                lanes = np.nonzero(ok[g])[0]
                out, at = np.unique(src[g, lanes], return_index=True); lanes = lanes[at]
                oc[r, g, s[g, lanes]] = new[g, lanes]; oc[r, g, out] = C - 1
        arrived = sent
    return {"y": oc.astype(np.float32)}

import numpy as np
from concourse.mybir import AluOpType as A, ActivationFunctionType as F

BF, FP, F16, I32, U16 = "bfloat16", "float32", "float16", "int32", "uint16"
S, L, B, U, RO = 2048, 128, 96, 32, 3
W = 2320
BIG = 4096.0
NENG = 8
FUSED, PLAIN = [2, 3], [0, 1]

SCRATCH = {}
for _n, _w, _d in [
        ("SK", S, BF), ("OC", 128, I32), ("CD", 384, I32), ("ND", 288, BF), ("CV", S, I32), ("JS", W, I32),
        ("CU", 384, U16), ("OU", 128, U16), ("SGU", 128, U16), ("CH", 384, F16), ("MS", 384, F16), ("S0L", 24, U16), ("S0Y", 8, U16),
        ("CY", 512, BF), ("M16", 384, F16), ("DM", 128, FP), ("ONES", S, BF), ("THR", 128, FP), ("D32", 128, FP), ("DR", S, BF), ("E", S, BF),
        ("HLF", 128, FP), ("HL", 128, BF), ("LO", 16, FP), ("IO", S, FP), ("INV0", S, FP), ("INV1", S, FP), ("INV2", S, FP),
        ("ML", 384, U16), ("MH", 384, F16), ("PN", S, BF), ("RN", S, BF),
        ("PL0", 128, U16), ("PL1", 128, U16), ("PL2", 128, U16), ("PT0", 128, FP), ("PT1", 128, FP), ("PT2", 128, FP),
        ("RL0", 128, U16), ("RL1", 128, U16), ("RL2", 128, U16), ("XS", S, BF), ("XG", S + 16, BF), ("XK", W, BF), ("XT", S, BF),
        ("X15", 128, BF), ("EE", S, BF), ("D1", 1536, BF), ("D1F", 512, FP), ("NF", 128, FP), ("NZ", 384, BF), ("BS", 128, BF), ("BT", 128, BF),
        ("BE", S, BF), ("AB", S, BF), ("CM", S, BF), ("NFM", 128, FP), ("KY", 128, FP), ("SC8", 128, FP), ("C8", 8, FP), ("ST8", 8, FP),
        ("DG", 1024, F16), ("EQ", 1024, F16), ("LU", 8, U16), ("LS", 8, U16), ("NV", 128, BF), ("NJ", 128, FP), ("OJ", 128, FP),
        ("ZB", 128, BF), ("ZF", 128, FP), ("DD", 128, FP), ("RD", 128, BF), ("UU", 128, FP), ("CN", 128, FP), ("WW", 128, FP), ("OF0", 128, FP),
        ("OFF", 128, BF), ("DQ", 128, FP), ("OL", 8, U16), ("SL0", 256, FP), ("SL1", 256, FP), ("ARR0", U, FP), ("ARR1", U, FP),
        ("RB0", U, FP), ("RB1", U, FP), ("ARB", U, BF), ("YY", W, FP)]:
    SCRATCH[_n] = ("sbuf", [128, _w], _d)
PARTS = {}
for _b, _d, _l in [
        ("GI", I32, [("TA", 128), ("TB", 128), ("TC", 128), ("W1", 128), ("W2", 128), ("W3", 128), ("W4", 128), ("T1", 128), ("T3", 128),
                     ("T2", 8), ("CI", 8), ("PI", 8), ("SI", 8), ("IP", 8), ("IQ", 8)]),
        ("GF", FP, [("LOF", 16), ("PO", 8), ("PV", 8), ("DCOL", 8), ("CYA", 8), ("CYB", 8), ("CYC", 8)]),
        ("GB", BF, [("ID", 128), ("I18", 128), ("I18N", 128), ("BLKW", 128), ("BLKN", 128), ("CCON", 128), ("SELW", 8), ("SEL2", 8)]),
        ("GH", F16, [("IH", 128), ("PM1", 128), ("PM4", 128), ("S0R", 128), ("TRI", 128), ("PH", 128), ("FS", 128), ("LOS", 128), ("LD", 128),
                     ("FT", 128), ("FM", 128), ("B16", 16), ("ONE16", 16), ("F4K", 16)])]:
    _o = 0
    for _n, _w in _l:
        PARTS[_n] = (_b, _o, {"IP": 1, "IQ": 1, "PO": 1, "PV": 1, "DCOL": 1, "CYA": 1, "CYB": 1, "CYC": 1, "B16": 8}.get(_n, _w))
        _o += _w
    SCRATCH[_b] = ("sbuf", [128, _o], _d)
for _k in range(8):
    SCRATCH["P%d" % _k] = ("psum", [128, 512], FP)
SEMAPHORES = ["cV", "cS", "cP", "cG", "dJ"] + ["d%d" % k for k in range(10)] + ["arr0", "arr1", "rin0", "rin1", "out0", "out1"]

TUNE = {"sc": 3.0, "rlat": 6.0, "hop": 0.12, "own": 0.06, "trials": 400}
ORDER = {}


def arrange(ops, pr):
    m, hop = len(ops), TUNE["hop"]
    succ = [[] for _ in range(m)]
    for i, o in enumerate(ops):
        for j in o["edges"]:
            succ[j].append(i)
    up = [0.0] * m
    for i in range(m - 1, -1, -1):
        o = ops[i]
        up[i] = o["cost"] + max([up[j] + (0.0 if ops[j]["edges"][i] == 0 and ops[j]["q"] == o["q"] else hop + o["lat"]) for j in succ[i]] + [o["lat"]])
    jit = pr["jit"] * np.random.default_rng(pr["seed"]).standard_normal(m)
    key = [up[i] + pr["b"].get(ops[i]["tag"], 0.0) + float(jit[i]) for i in range(m)]
    left = [len(o["edges"]) for o in ops]
    ready = [i for i in range(m) if not left[i]]
    slots = {k: [] for k in "VSPGY"}
    at, end, on = [0.0] * m, [0.0] * m, [""] * m
    while ready:
        i = max(ready, key=lambda i: (key[i], -i))
        ready.remove(i)
        for j in succ[i]:
            left[j] -= 1
            if not left[j]:
                ready.append(j)
        o = ops[i]
        best = None
        for q in o["q"]:
            s = 0.0
            for j, e in o["edges"].items():
                if on[j] == q and e == 0:
                    s = max(s, at[j] + ops[j]["cost"])
                else:
                    s = max(s, end[j] + (hop if on[j] != q else TUNE["own"]))
            for (a, b) in slots[q]:
                if s + o["cost"] <= a:
                    break
                s = max(s, b)
            pen = s + o["cost"] + (pr["pv"] if q == "V" and len(o["q"]) > 1 else 0.0)
            if best is None or pen < best[0] - 1e-9:
                best = (pen, s, q)
        _, s, q = best
        on[i], at[i], end[i] = q, s, s + o["cost"] + o["lat"]
        slots[q].append((s, s + o["cost"]))
        slots[q].sort()
    return max(end), at, on


def order_of(ops):
    if "at" not in ORDER:
        r = np.random.default_rng(1)
        best, pr = None, {"pv": 1.5, "jit": 0.0, "seed": 0, "b": {}}
        for k in range(TUNE["trials"]):
            p = dict(pr, b=dict(pr["b"]))
            if k:
                c = int(r.integers(4))
                if c == 0:
                    p["seed"], p["jit"] = int(r.integers(1000000)), float(r.choice([0.0, 0.2, 0.5, 1.0]))
                elif c == 1:
                    p["pv"] = float(r.choice([0.3, 0.6, 1.0, 1.5, 2.0]))
                else:
                    p["b"][str(r.choice(["i0", "i1", "i2", "p0", "p1", "p2", "n0", "n1", "n2", "h0", "h1", "j0", "j1", "y"]))] = float(3 - 14 * r.random())
            e = arrange(ops, p)
            if best is None or e[0] < best[0]:
                best, pr = e, p
        ORDER["end"], ORDER["at"], ORDER["on"] = best
    return ORDER["at"], ORDER["on"]


def rank_program(g, core, T, topo):
    cores = list(T.cores)
    n = len(cores)

    def relay_of(r):
        src, dst = cores[r], cores[(r + 1) % n]
        c = [x for x in topo.cores_of(src) if x != src and topo.may_write(x, dst)]
        c.sort(key=lambda x: (topo.die(x) != topo.die(src), x))
        return c[0]

    def emask(a, b):
        e = topo.engines(a, b)[:NENG]
        return sum(1 << x for x in e), len(e)

    rank = T.rank_of(core)
    if rank is None:
        for r in range(n):
            if relay_of(r) == core:
                dst = cores[(r + 1) % n]
                _, nin = emask(cores[r], core)
                m, k = emask(core, dst)
                rid, pid = topo.addr(dst, core)
                for t in range(RO - 1):
                    g.wait_ge(T.sem["rin%d" % t], nin)
                    g.remote_dma(T["ARR%d" % t][:, :], T["RB%d" % t][:, :], T.sem["arr%d" % t], T.sem["out%d" % t], pid, rid, m)
                for t in range(RO - 1):
                    g.wait_ge(T.sem["out%d" % t], k)
        return

    Q = {"V": g.vector, "S": g.scalar, "P": g.tensor, "G": g, "Y": g.sync}
    CS = {"V": "cV", "S": "cS", "P": "cP", "G": "cG"}
    ops, acc, tag = [], {}, [""]

    def R(name, lo=0, hi=None, st=1):
        if name in PARTS:
            b, o, w = PARTS[name]
            return (b, o + lo, o + (w if hi is None else hi), st)
        return (name, lo, SCRATCH[name][1][-1] if hi is None else hi, st)

    def ap(r):
        return T[r[0]][:, r[1]:r[2]:r[3]] if r[3] != 1 else T[r[0]][:, r[1]:r[2]]

    def psum(name):
        return SCRATCH[name][0] == "psum"

    def width(r):
        return (r[2] - r[1] + r[3] - 1) // r[3]

    def two(*rs):
        return all(SCRATCH[r[0]][2] in (BF, F16, U16) for r in rs)

    def overlap(a, b):
        if psum(a[0]):
            return True
        if a[1] >= b[2] or b[1] >= a[2]:
            return False
        return not (a[3] == b[3] and a[3] > 1 and (a[1] - b[1]) % a[3])

    def add(q, fn, reads, writes, cost, chain=False, kind="c", lat=0.0, extra=None):
        me, edges = len(ops), {}
        mine = [(r, "r") for r in reads] + [(r, "w") for r in writes]
        for rr, k in mine:
            for (o, ok, j) in acc.get(rr[0], []):
                if j == me or not overlap(rr, o):
                    continue
                if k == "r" and ok == "r":
                    if psum(rr[0]):
                        edges[j] = max(edges.get(j, 0), 0)
                    continue
                e = 0 if k == "w" and chain else 1
                if psum(rr[0]) and q == "P" and ops[j]["q"] == "P" and (rr[1] >= o[2] or o[1] >= rr[2]):
                    e = 0
                edges[j] = max(edges.get(j, 0), e)
        for rr, k in mine:
            keep = []
            for e in acc.get(rr[0], []):
                o = e[0]
                cov = rr[1] <= o[1] and o[2] <= rr[2] and (rr[3] == 1 or (rr[3] == o[3] and (rr[1] - o[1]) % rr[3] == 0))
                if k == "w" and e[2] != me and (cov or (psum(rr[0]) and ops[e[2]]["q"] != "P")):
                    continue
                keep.append(e)
            keep.append((rr, k, me))
            acc[rr[0]] = keep
        ops.append({"tag": tag[0], "q": q, "fn": fn, "cost": cost, "edges": edges, "kind": kind, "lat": lat, "x": extra})

    def op(q, fn, reads, writes, cyc, chain=False):
        add(q, fn, reads, writes, (0.02 + max(cyc, 64) * 0.00083) * 1.2, chain)

    def dma(q, out, in_, reads, writes, lat, group=None):
        add(q, lambda e, z: e.dma_start(out, in_), reads, writes, 0.1, kind="d", lat=lat, extra=group)

    def copy(q, o, i, scale=1.0, bias=0.0):
        def f(e, z):
            if z == "V":
                if scale == 1.0 and bias == 0.0:
                    return e.tensor_copy(ap(o), ap(i))
                return e.tensor_scalar(ap(o), ap(i), float(scale), float(bias), A.mult, A.add)
            return e.activation(ap(o), ap(i), F.Copy if bias == 0.0 else F.Identity, bias=float(bias), scale=float(scale))
        op(q, f, [i], [o], width(i))

    def relu(q, o, i):
        op(q, lambda e, z: e.tensor_scalar(ap(o), ap(i), 0.0, None, A.max) if z == "V" else e.activation(ap(o), ap(i), F.Relu), [i], [o], width(i))

    def ts(o, i, s1, op0, s2=None, op1=None):
        rd, a1, a2 = [i], s1, s2
        if isinstance(s1, tuple):
            rd.append(s1)
            a1 = ap(s1)
        if isinstance(s2, tuple):
            rd.append(s2)
            a2 = ap(s2)
        c = width(i) * (0.5 if two(o, i) else 1)
        if op1 is None:
            op("V", lambda e, z: e.tensor_scalar(ap(o), ap(i), a1, None, op0), rd, [o], c)
        else:
            op("V", lambda e, z: e.tensor_scalar(ap(o), ap(i), a1, a2, op0, op1), rd, [o], c)

    def tt(o, a, b, o_):
        op("V", lambda e, z: e.tensor_tensor(ap(o), ap(a), ap(b), o_), [a, b], [o], width(o) * (1 if psum(a[0]) or psum(b[0]) else 2))

    def fill(o, v, q="V"):
        if q == "G":
            op(q, lambda e, z: e.iota(ap(o), [[0, width(o)]], int(v), 0, allow_small_or_imprecise_dtypes=True), [], [o], 150 + 2 * width(o))
        else:
            op(q, lambda e, z: e.memset(ap(o), v), [], [o], width(o) * (0.5 if two(o) else 1))

    def scan(o, a, b, op0, op1):
        op("V", lambda e, z: e.tensor_tensor_scan(ap(o), ap(a), ap(b), 0.0, op0, op1), [a, b], [o], width(o) * (0.5 if two(o, a, b) else 1))

    def mm(o, l, r, start=True, stop=True):
        op("P", lambda e, z: e.matmul(ap(o), ap(l), ap(r), start, stop), [l, r], [o], max(min(64, width(l)), width(r)) * 0.86, chain=not start)

    def gath(q, o, win, lst):
        op(q, lambda e, z: e.tensor_copy(ap(o), ap(win).indirect(ap(lst))) if z == "V" else
           e.activation(ap(o), ap(win).indirect(ap(lst)), F.Copy), [win, lst], [o], 50 + 1.5 * width(o))

    def scat(win, lst, i):
        op("V", lambda e, z: e.tensor_copy(ap(win).indirect(ap(lst)), ap(i)), [lst, i], [win], 50 + TUNE["sc"] * width(i))

    def place(win, lst, i):
        op("VS", lambda e, z: e.tensor_copy(ap(win).indirect(ap(lst)), ap(i)) if z == "V" else
           e.activation(ap(win).indirect(ap(lst)), ap(i), F.Silu), [lst, i], [win], 50 + TUNE["sc"] * width(i))

    def iota(o, pat, base, cm, fl=False):
        if fl:
            op("G", lambda e, z: e.iota(ap(o), pat, base, cm, allow_small_or_imprecise_dtypes=True), [], [o], 150 + 2 * width(o))
        else:
            op("G", lambda e, z: e.iota(ap(o), pat, base, cm), [], [o], 150 + 2 * width(o))

    def wrap(bank, src, k0, k1):
        for r in range(16):
            mm(R(bank, 0, k1 - k0), R("DR", 128 * r, 128 * r + 128), R(src, 16 * k0 + r, 16 * k1, 16), r == 0, r == 15)

    h = S // 2
    dma("Y", T.CD[:, 0:128], T.cards[:, 0:128], [], [R("CD", 0, 128)], 2.4)
    dma("S", T.SK[:, 0:h], T.skill[:, 0:h], [], [R("SK", 0, h)], 3.5)
    dma("Y", T.OC[:, :], T.occ[:, :], [], [R("OC")], 2.6)
    dma("S", T.SK[:, h:S], T.skill[:, h:S], [], [R("SK", h, S)], 4.5)
    dma("Y", T.ND[:, :], T.need[:, :], [], [R("ND")], 5.0)
    dma("Y", T.CD[:, 128:384], T.cards[:, 128:384], [], [R("CD", 128, 384)], 5.5)
    dma("Y", T.CV[:, :], T.cover[:, :], [], [R("CV")], 9.0)
    for q in range(16):
        dma("Y", T.JS[q:128:16, 0:S], T.occ[:, :], [], [R("JS", q * 128, q * 128 + 128)], 12.0, ("dJ", 256))

    iota(R("IP"), [[0, 1]], 0, 1)
    iota(R("HLF"), [[1024, 128]], 0, 0, True)
    iota(R("LOF"), [[64, 16]], 64, 0, True)
    iota(R("W1"), [[-16, 8], [0, 16]], 0, 1)
    iota(R("W2"), [[-1, 128]], 0, 1)
    iota(R("W3"), [[0, 8], [-1, 16]], 0, 1)
    iota(R("W4"), [[-16, 8], [1, 16]], -15, 1)
    iota(R("DCOL"), [[0, 1]], 2050, 2, True)
    iota(R("D32"), [[1, 128]], 128, 0, True)
    fill(R("ONES"), 1.0)
    fill(R("DR"), 0.0, "G")
    fill(R("D1"), 0.0, "G")
    fill(R("D1F"), 0.0, "G")
    op("G", lambda e, z: e.affine_select(ap(R("E")), ap(R("ONES")), [[-1, 128], [0, 16]], A.is_equal, 0.0, 0, 1), [R("ONES")], [R("E")], 200 + 2 * S)
    ts(R("T2"), R("W1", 0, 128, 16), 1, A.arith_shift_right)
    ts(R("SEL2"), R("T2"), 0.0, A.is_equal, 1.0 / 64, A.mult)
    for r in range(16):
        copy("VS", R("DR", 128 * r + r, 128 * r + 128, 16), R("SEL2"))
    ts(R("IQ"), R("IP"), 1, A.bitwise_and)
    copy("V", R("PO"), R("IQ"))
    copy("V", R("PV"), R("IQ"), -1.0, 1.0)
    ts(R("HL"), R("HLF"), R("PV"), A.mult)
    ts(R("LO"), R("LOF"), R("PO"), A.mult)

    def io_col(i):
        o, b = R("IO", i, S, 16), R("LO", i, i + 1)
        op("VS", lambda e, z: e.tensor_scalar(ap(o), ap(R("HL")), ap(b), None, A.add) if z == "V" else
           e.activation(ap(o), ap(R("HL")), F.Identity, bias=ap(b)), [R("HL"), b], [o], 128)

    for i in range(16):
        io_col(i)
    copy("V", R("CU", 0, 128), R("CD", 0, 128))
    ts(R("TA"), R("CD", 0, 128), 127, A.bitwise_and)
    ts(R("TB"), R("CD", 0, 128), 7, A.arith_shift_right)
    ts(R("TC"), R("TA"), 16.0, A.mult)
    tt(R("TA"), R("TC"), R("TB"), A.add)
    copy("V", R("SGU"), R("TA"))
    copy("V", R("OU"), R("OC"))
    ts(R("ID"), R("W2"), 0.0, A.is_equal)
    ts(R("T1"), R("W1"), 4, A.arith_shift_right)
    ts(R("BLKW"), R("T1"), 0.0, A.is_equal, 512.0, A.mult)
    fill(R("XG", 0, 1), BIG)
    fill(R("XK", 0, 1), 0.0)
    fill(R("XK", S + 1, W), 0.0)
    ts(R("SK", 0, h), R("SK", 0, h), 1.0 / 64, A.max)
    ts(R("SK", h, S - 1), R("SK", h, S - 1), 1.0 / 64, A.max)
    for c in range(4):
        gath("VS", R("XS", 512 * c, 512 * c + 512), R("SK"), R("OU", 32 * c, 32 * c + 32))

    def needs(t):
        copy("VS", R("D1", 0, 1536, 16), R("ND", B * t, B * t + B), -1.0)
        if t < RO - 1:
            copy("VS", R("NF", 0, B), R("ND", B * t, B * t + B))

    needs(0)
    mm(R("P7", 0, 288), R("BLKW"), R("ND"))
    for t in range(RO):
        ts(R("NZ", 128 * t, 128 * t + B), R("P7", B * t, B * t + B), 0.0, A.is_equal, 512.0, A.mult)
    fill(R("NZ", B, 128), 512.0)
    fill(R("NF", B, 128), 0.0)
    copy("V", R("CU", 128, 384), R("CD", 128, 384))
    copy("V", R("CH"), R("CD"))
    ts(R("S0R"), R("W1"), 0.0, A.is_equal)
    ts(R("B16"), R("T1", 0, 128, 16), 0.0, A.is_equal)
    ts(R("T3"), R("W3"), 15, A.bitwise_and)
    for t in range(RO):
        ts(R("M16", 128 * t, 128 * t + 128), R("T3"), 0.0, A.is_equal)
    for t in range(RO):
        mm(R("P6", 128 * t, 128 * t + 128), R("CH", 128 * t, 128 * t + 128), R("S0R"))
    tt(R("MS"), R("P6", 0, 384), R("M16"), A.mult)
    for t in range(RO):
        mm(R("P6", 8 * t, 8 * t + 8), R("MS", 128 * t, 128 * t + 128), R("B16"))
    copy("V", R("S0L"), R("P6", 0, 24))
    copy("V", R("S0Y"), R("P6", 16, 24), 1.0, 1.0)
    for t in range(RO):
        gath("V", R("ML", 128 * t, 128 * t + 128), R("CV"), R("S0L", 8 * t, 8 * t + 8))
        copy("V", R("MH", 128 * t, 128 * t + 128), R("ML", 128 * t, 128 * t + 128))
    ts(R("PM1"), R("W4"), 0.0, A.is_equal, -1.0, A.mult)
    ts(R("PM4"), R("W4"), 0.0, A.is_equal, 4096.0, A.mult)
    ts(R("SELW"), R("T1", 0, 128, 16), 0.0, A.is_equal, 67108864.0, A.mult)
    ts(R("BLKN"), R("T1"), 0.0, A.is_equal, -262144.0, A.mult)
    ts(R("I18"), R("W2"), 0.0, A.is_equal, 262144.0, A.mult)
    ts(R("I18N"), R("W2"), 0.0, A.is_equal, -262144.0, A.mult)
    ts(R("IH"), R("W2"), 0.0, A.is_equal)
    ts(R("TRI"), R("W2"), 0.0, A.is_gt)
    ts(R("DM"), R("T3"), 0.0, A.is_equal, R("DCOL"), A.mult)
    ts(R("ONE16"), R("W2", 0, 16), 0.0, A.mult, 1.0, A.add)
    ts(R("F4K"), R("W2", 0, 16), 0.0, A.mult, 4096.0, A.add)
    fill(R("CCON"), -4980736.0)
    fill(R("THR"), 0.0)
    fill(R("THR", 0, 128, 16), -9.0e9)
    fill(R("ZB"), 0.0)
    fill(R("ZF"), 2047.0)
    fill(R("JS", S, W), 0)
    fill(R("YY", 0, 1), 2047.0)
    fill(R("YY", S + 1, W), 2047.0)
    ts(R("CYA"), R("W2", 0, 1), 0.0, A.is_equal, 2048.0, A.mult)
    ts(R("CYB"), R("W2", 0, 1), 1.0, A.is_equal, -1.0, A.mult)
    tt(R("CYC"), R("CYA"), R("CYB"), A.add)
    ts(R("CY"), R("ONES", 0, 512), R("CYC"), A.mult)

    def lists(t):
        tag[0] = "i%d" % t
        for p in range(8):
            place(R("INV%d" % t), R("CU", 128 * t + 16 * p, 128 * t + 16 * p + 16), R("IO", 256 * p, 256 * p + 256))
        tag[0] = "p%d" % t
        for c in range(4):
            gath("VS", R("PN", 512 * c, 512 * c + 512), R("INV%d" % t), R("ML", 128 * t + 32 * c, 128 * t + 32 * c + 32))
        wrap("P7", "PN", 0, 128)
        copy("V", R("PL%d" % t), R("P7", 0, 128))
        if t < RO - 1:
            copy("V", R("PH"), R("P7", 0, 128))
            mm(R("P7", 0, 128), R("PH"), R("PM1"), True, False)
            mm(R("P7", 0, 128), R("MH", 128 * t, 128 * t + 128), R("PM4"), False, True)
            copy("VS", R("PT%d" % t), R("P7", 0, 128), 1.0, 2050.0)
        else:
            mm(R("P7", 0, 128), R("MH", 128 * t, 128 * t + 128), R("PM1"))
            copy("VS", R("PT%d" % t), R("P7", 0, 128), 1.0, 2049.0)
        tag[0] = "n%d" % t
        for c in range(4):
            if t < RO - 1:
                gath("VS", R("RN", 512 * c, 512 * c + 512), R("INV%d" % t), R("CU", 128 * t + 128 + 32 * c, 128 * t + 160 + 32 * c))
            else:
                copy("VS", R("RN", 512 * c, 512 * c + 512), R("INV2", 512 * c, 512 * c + 512))
        wrap("P7", "RN", 0, 128)
        copy("V", R("RL%d" % t), R("P7", 0, 128))
        tag[0] = ""

    lists(0)

    for t in range(RO):
        win, lst = (R("XS"), "SGU") if t == 0 else (R("XK"), "RL%d" % (t - 1))
        PL, last = "PL%d" % t, t == RO - 1
        for c in range(4):
            gath("VS", R("XG", 1 + 512 * c, 513 + 512 * c), win, R(lst, 32 * c, 32 * c + 32))
        if t > 0:
            a = R("ARR%d" % (t - 1))
            copy("VS", R("ARB"), a)
            copy("VS", R("D1F", 0, 512, 16), a, -1.0)
            if not last:
                copy("VS", R("NF", B, 128), a)
            mm(R("P5", 0, U), R("BLKW"), R("ARB"))
            ts(R("NZ", 128 * t + B, 128 * t + 128), R("P5", 0, U), 0.0, A.is_equal, 512.0, A.mult)
        for c in range(4):
            mm(R("P%d" % c), R("ID"), R("XG", 1 + 512 * c, 513 + 512 * c), True, False)
        x0 = R("XG", 1, S, 16)
        ts(R("BS"), x0, 0.0, A.is_equal, 512.0, A.mult)
        mm(R("P6", 0, 128), x0, R("ID"))
        copy("VS", R("BT"), R("P6", 0, 128))
        for c in range(4):
            x15 = R("XG", 16 + 512 * c, 513 + 512 * c, 16)
            if not last:
                copy("VS", R("X15", 32 * c, 32 * c + 32), x15)
            fill(x15, BIG)
            d1 = R("D1", 512 * c, 512 * c + 512) if c < 3 else R("D1F")
            scan(R("EE", 512 * c, 512 * c + 512), R("XG", 512 * c, 512 * c + 512), d1, A.add, A.min)
            mm(R("P%d" % c), R("BLKW"), R("EE", 512 * c, 512 * c + 512), False, True)
            relu("VS", R("XK", 1 + 512 * c, 513 + 512 * c), R("P%d" % c))
        for c in FUSED:
            mm(R("P4"), R("BT"), R("E", 512 * c, 512 * c + 512))
            copy("VS", R("BE", 512 * c, 512 * c + 512), R("P4"))
        for c in PLAIN:
            mm(R("P%d" % c), R("BT"), R("E", 512 * c, 512 * c + 512))

        def fused(c):
            m, b, p = R("CM", 512 * c, 512 * c + 512), R("BE", 512 * c, 512 * c + 512), R(PL, 32 * c, 32 * c + 32)
            op("V", lambda e, z: e.tensor_tensor(ap(m), ap(R("XK")).indirect(ap(p)), ap(b), A.is_ge), [R("XK"), p, b], [m], 50 + 1.5 * 512)

        for c in PLAIN:
            gath("S", R("AB", 512 * c, 512 * c + 512), R("XK"), R(PL, 32 * c, 32 * c + 32))
        for c in FUSED:
            fused(c)
        for c in PLAIN:
            tt(R("CM", 512 * c, 512 * c + 512), R("AB", 512 * c, 512 * c + 512), R("P%d" % c), A.is_ge)
        if not last:
            tag[0] = "h%d" % t
            for i in range(16):
                mm(R("P5", 0, 128), R("ID"), R("XG", 1 + i, S, 16) if i < 15 else R("X15"), i == 0, i == 15)
            tt(R("DD"), R("NF"), R("P5", 0, 128), A.subtract)
            relu("VS", R("RD"), R("DD"))
            mm(R("P5", 0, 128), R("BLKW"), R("RD"))
            ts(R("UU"), R("P5", 0, 128), 0.1, A.is_gt)
            scan(R("CN"), R("ONES", 0, 128), R("UU"), A.mult, A.add)
            ts(R("WW"), R("UU"), -1000.0, A.mult, 999.0, A.add)
            tt(R("OF0"), R("CN"), R("WW"), A.add)
            tt(R("OFF"), R("OF0"), R("D32"), A.min)
            wrap("P5", "OFF", 0, 8)
            sl = "SL%d" % t
            ts(R("DQ"), R("DD"), 0.0, A.max, 8388608.0, A.add)
            fill(R(sl), 0.0)
            copy("V", R("OL"), R("P5", 0, 8), 32.0, 0.0)

            def put(e, z, sl=sl):
                return e.tensor_scalar(ap(R(sl)).indirect(ap(R("OL"))), ap(R("DQ")), 1.0, -8388608.0, A.mult, A.add)
            op("V", put, [R("OL"), R("DQ")], [R(sl)], 50 + TUNE["sc"] * 128)
            rl = relay_of(rank)
            m, k = emask(core, rl)
            rid, pid = topo.addr(rl, core)
            _, ka = emask(relay_of((rank - 1) % n), core)

            def send(e, z, t=t, sl=sl, rid=rid, pid=pid, m=m):
                return e.remote_dma(T["RB%d" % t][:, :], ap(R(sl, 0, U)), T.sem["rin%d" % t], T.sem["out%d" % t], pid, rid, m)
            add("G", send, [R(sl, 0, U)], [R("ARR%d" % t)], 0.6, kind="m", lat=TUNE["rlat"], extra=("arr%d" % t, ka, "out%d" % t, k))
            tag[0] = ""
            needs(t + 1)
            lists(t + 1)
        mm(R("P6", 0, 128), R("ONES", 0, 128), R("CCON"), True, False)
        mm(R("P6", 0, 128), R("BS"), R("BLKN"), False, False)
        mm(R("P6", 0, 128), R("NZ", 128 * t, 128 * t + 128), R("BLKN"), False, False)
        for i in range(16):
            mm(R("P6", 15 - i, 128, 16), R("CM", i, S, 16), R("SELW"), False, i == 15)
        tt(R("NFM"), R("P6", 0, 128), R("THR"), A.is_lt)
        tt(R("KY"), R("P6", 0, 128), R("PT%d" % t), A.min)
        scan(R("SC8"), R("NFM"), R("KY"), A.mult, A.max)
        if last:
            copy("V", R("C8"), R("SC8", 15, 128, 16), -1.0, 2050.0)
        else:
            copy("V", R("CI"), R("SC8", 15, 128, 16))
            ts(R("PI"), R("CI"), 4095, A.bitwise_and)
            copy("V", R("C8"), R("PI"), -1.0, 2050.0)
        for q in range(8):
            ts(R("DG", 128 * q, 128 * q + 128), R("IH"), R("C8", q, q + 1), A.mult)
        for b in range(2):
            mm(R("P%d" % (4 + b)), R("TRI"), R("DG", 512 * b, 512 * b + 512))
        for q in range(8):
            ts(R("EQ", 128 * q, 128 * q + 128), R("P%d" % (4 + q // 4), 128 * (q % 4), 128 * (q % 4) + 128), R("C8", q, q + 1), A.is_equal)
        for q in range(8):
            o = R("P6", 16 * q, 16 * q + 16)
            mm(o, R("DG", 128 * q, 128 * q + 128), R("ONE16"), True, False)
            mm(o, R("EQ", 128 * q, 128 * q + 128), R("F4K"), False, True)
        tt(R("FM"), R("P6", 0, 128), R("DM"), A.min)
        mm(R("P3", 0, 8), R("FM"), R("B16"))
        copy("V", R("LU"), R("P3", 0, 8))
        if not last:
            gath("V", R("NV"), R("XK"), R("LU"))
            tag[0] = "j%d" % t
            mm(R("P2", 0, 128), R("I18"), R("XK", 1, S, 16))
            gath("V", R("OJ"), R("JS"), R("S0L", 8 * t, 8 * t + 8))
            tt(R("OJ"), R("OJ"), R("P2", 0, 128), A.min)
            ts(R("SI"), R("CI"), 12, A.arith_shift_right)
            copy("V", R("ST8"), R("SI"))
            for q in range(8):
                ts(R("FS", 16 * q, 16 * q + 16), R("M16", 0, 16), R("ST8", q, q + 1), A.mult)
            ts(R("LOS"), R("P6", 0, 128), 2049.0, A.is_ge)
            tt(R("LD"), R("LOS"), R("DM"), A.mult)
            tt(R("FT"), R("FS"), R("LD"), A.max)
            mm(R("P2", 0, 8), R("FT"), R("B16"))
            copy("V", R("LS"), R("P2", 0, 8))
            gath("V", R("NJ"), R("JS"), R("LS"))
            tt(R("NJ"), R("NJ"), R("OJ"), A.max)
            scat(R("JS"), R("S0L", 8 * t, 8 * t + 8), R("NJ"))
            tag[0] = ""
            scat(R("XK"), R("LU"), R("ZB"))
            xd = R("XK", 1, S, 16)
            tt(xd, xd, R("NV"), A.add)
        else:
            tag[0] = "y"
            for c in range(4):
                gath("VS", R("XT", 512 * c, 512 * c + 512), R("XK"), R("RL2", 32 * c, 32 * c + 32))
            for c in range(4):
                mm(R("P%d" % c), R("ONES", 0, 128), R("CY"), True, False)
                mm(R("P%d" % c), R("I18N"), R("XT", 512 * c, 512 * c + 512), False, True)
                tt(R("YY", 1 + 512 * c, 513 + 512 * c), R("JS", 512 * c, 512 * c + 512), R("P%d" % c), A.max)
            tag[0] = ""
            gath("V", R("NJ"), R("YY"), R("LU"))
            scat(R("YY"), R("LU"), R("ZF"))
            gath("V", R("OJ"), R("YY"), R("S0Y"))
            tt(R("NJ"), R("NJ"), R("OJ"), A.min)
            scat(R("YY"), R("S0Y"), R("NJ"))
            for c in range(2):
                dma("YS"[c], T.y[:, h * c:h * c + h], T.YY[0:128:16, 1 + h * c:1 + h * c + h], [R("YY", 1 + h * c, 1 + h * c + h)], [], 2.0)

    at, on = order_of(ops)
    m = len(ops)
    cnt = {k: 0 for k in CS}
    known = {k: {} for k in Q}
    total = {}
    done = [None] * m
    nd = 0
    for i in sorted(range(m), key=lambda i: (at[i], i)):
        o = ops[i]
        q = on[i]
        need = {}
        for j, e in o["edges"].items():
            if e == 0 and on[j] == q and ops[j]["kind"] == "c" and o["kind"] == "c":
                continue
            need[done[j][0]] = max(need.get(done[j][0], 0), done[j][1])
        for s in sorted(need):
            if known[q].get(s, 0) < need[s]:
                Q[q].wait_ge(T.sem[s], need[s])
                known[q][s] = need[s]
        ins = o["fn"](Q[q], q)
        if o["kind"] == "c":
            cnt[q] += 1
            ins.then_inc(T.sem[CS[q]], 1)
            done[i] = (CS[q], cnt[q])
        elif o["kind"] == "d":
            if o["x"] is None:
                done[i] = ("d%d" % nd, 16)
                nd += 1
            else:
                done[i] = o["x"]
            ins.then_inc(T.sem[done[i][0]], 16)
        else:
            done[i] = (o["x"][0], o["x"][1])
            total[o["x"][2]] = o["x"][3]
        total[done[i][0]] = max(total.get(done[i][0], 0), done[i][1])
    for s in sorted(total):
        if known["G"].get(s, 0) < total[s]:
            g.wait_ge(T.sem[s], total[s])
